import numpy as np
import ml_dtypes


def mxq(x, axis, fmt="e4m3"):
    dtype, down = {"e4m3": (ml_dtypes.float8_e4m3fn, 7), "e5m2": (ml_dtypes.float8_e5m2, 14)}[fmt]
    v = np.moveaxis(np.asarray(x, np.float32).astype(ml_dtypes.bfloat16).astype(np.float64), axis, -1)
    blocks = v.reshape(v.shape[:-1] + (-1, 32))
    amax = np.abs(blocks).max(-1, keepdims=True)
    byte = np.maximum(np.where(amax > 0, np.frexp(amax)[1] - 1 + 127, 0) - down, 1)
    scale = np.exp2(byte - 127.0)
    codes = (blocks / scale).astype(np.float32).astype(dtype).astype(np.float64)
    return np.moveaxis((codes * scale).reshape(v.shape), -1, axis)


WIDE = False


def mx_kscale(k):
    if not WIDE:
        return np.ones(k)
    levels = np.array([10, -10, 5, -5, 0])
    if k % 512:
        return np.exp2(np.random.permutation(np.resize(levels, k // 32))).repeat(32)
    a = np.empty((k // 512, 16))
    for p in range(k // 512):
        a[p, :8] = np.random.permutation(np.resize(levels, 8))
        for g in range(8):
            far = levels[np.abs(levels - a[p, g]) >= 10]
            a[p, g + 8] = far[np.random.randint(len(far))]
    return np.exp2(a.ravel()).repeat(32)


def f64(x):
    return np.asarray(x).astype(np.float64)


def striped(idx):
    return np.tile(idx.reshape(-1, 16).T, (8, 1)).astype(np.uint16)


def unstriped(offs):
    return offs[:16].T.reshape(-1).astype(np.int64)


def striped8(idx):
    return np.concatenate([x.reshape(-1, 16).T for x in idx]).astype(np.uint16)


def runs(offs, k):
    lists = np.stack([offs[16 * r : 16 * r + 16].T.reshape(-1) for r in range(8)]).astype(np.int64)
    return lists[np.arange(k) % 512 // 64]


def pack_weight(w):
    k, n = w.shape
    w = f64(np.asarray(w, np.float32).astype(ml_dtypes.bfloat16)).reshape(k // 32, 32, n)
    amax = np.abs(w).max(1)
    byte = np.clip(np.where(amax > 0, np.frexp(amax)[1] - 1 + 127 - 7, 1), 1, 254)
    scaled = (w * np.exp2(127.0 - byte)[:, None, :]).reshape(k, n).astype(np.float32)
    words = np.ascontiguousarray(scaled.reshape(k // 512, 128, 4, n).transpose(0, 1, 3, 2)).astype(ml_dtypes.float8_e4m3fn).view(np.uint8)
    return words, np.ascontiguousarray(byte.astype(np.uint8).reshape(k // 512, 16, n))


def unpack_weight(words, scales):
    g, p, n, _ = words.shape
    vals = np.ascontiguousarray(words).view(ml_dtypes.float8_e4m3fn).astype(np.float64) * np.repeat(np.exp2(scales.astype(np.float64) - 127.0), 8, axis=1)[..., None]
    return vals.transpose(0, 1, 3, 2).reshape(g * 512, n)


def sigmoid(v):
    return 1.0 / (1.0 + np.exp(-np.maximum(v, -700.0)))


K, T, S, G, H, W, C = 512, 1024, 256, 2048, 512, 128, 512


def setup_inputs():
    n = np.random.standard_normal
    s = mx_kscale(K)[:, None]
    packed_xT = pack_weight(n((K, T)) * s)
    packed_dT = pack_weight(n((K, G)) / s)
    perm = np.random.permutation(S)
    perm2 = np.random.permutation(S)
    perm3 = np.random.permutation(S)
    perm4 = np.random.permutation(S)
    return {
        "x_words": packed_xT[0],
        "x_scales": packed_xT[1],
        "d_words": packed_dT[0],
        "d_scales": packed_dT[1],
        "sl": np.random.uniform(1.0, 2.0, (H, 1)).astype(np.float32),
        "th": (0.5 * n((H, 1))).astype(np.float32),
        "gs": (np.random.uniform(0.5, 1.5, (K, 1)) / s).astype(np.float32),
        "offs": striped(np.random.permutation(T)[:S]),
        "k1": striped8(np.random.randint(0, G, (8, H))),
        "two": striped(np.random.permutation(T)[:S]),
        "k2": striped8(np.random.randint(0, G, (8, H))),
        "hz": striped8(np.random.randint(0, T, (8, S))),
        "k3": striped8(np.random.randint(0, G, (8, H))),
        "n1": striped(perm[:W]),
        "n2": striped(perm[W:]),
        "n3": striped(perm2[:W]),
        "n4": striped(perm2[W:]),
        "n5": striped(np.random.permutation(S)),
        "cand": striped(np.random.permutation(T)[:C]),
        "n6": striped(perm3[:W]),
        "n7": striped(perm3[W:]),
        "n8": striped(perm4[:W]),
        "n9": striped(perm4[W:]),
        "n10": striped(np.random.permutation(S)),
    }


def reference(x_words, x_scales, d_words, d_scales, sl, th, gs, offs, k1, two, k2, hz, k3, n1, n2, n3, n4, n5, cand, n6, n7, n8, n9, n10):
    x_cand = unpack_weight(x_words, x_scales)[:, unstriped(cand)]
    d_k1 = unpack_weight(d_words, d_scales)[np.arange(K)[:, None], runs(k1, K)]
    xq = unpack_weight(x_words, x_scales)[:, unstriped(offs)]
    d_k2 = unpack_weight(d_words, d_scales)[np.arange(K)[:, None], runs(k2, K)]
    x_two = unpack_weight(x_words, x_scales)[:, unstriped(two)]
    d_k3 = unpack_weight(d_words, d_scales)[np.arange(K)[:, None], runs(k3, K)]
    x_hz = unpack_weight(x_words, x_scales)[np.arange(K)[:, None], runs(hz, K)]
    h = 0.0625 * (d_k1.T @ xq + d_k2.T @ x_two + d_k3.T @ x_hz)
    pa = h[:, unstriped(n1)]
    pb = h[:, unstriped(n2)]
    rb = np.minimum(pa, pb)
    ra = np.maximum(pa, pb)
    ua = np.zeros((H, S))
    ua[:, unstriped(n3)] = ra
    ub = ua.copy()
    ub[:, unstriped(n4)] = rb
    sg = sigmoid(f64(sl) * (ub[:, unstriped(n5)] - f64(th)))
    z = f64(gs) * (ub * sg)
    s = 0.0625 * ((x_cand.T @ mxq(z, 0, "e4m3")))
    pa2 = s[:, unstriped(n6)]
    pb2 = s[:, unstriped(n7)]
    rb2 = np.maximum(pa2, pb2)
    ua2 = np.zeros((C, S))
    ua2[:, unstriped(n8)] = pb2
    ub2 = ua2.copy()
    ub2[:, unstriped(n9)] = rb2
    return ub2 - s[:, unstriped(n10)]

@@ -1,0 +1,248 @@
+from contextlib import ExitStack
+
+import concourse.mybir as mybir
+from concourse.masks import make_identity
+
+F32 = mybir.dt.float32
+BF16 = mybir.dt.bfloat16
+I32 = mybir.dt.int32
+U32 = mybir.dt.uint32
+U16 = mybir.dt.uint16
+U8 = mybir.dt.uint8
+FP8X4 = mybir.dt.float8_e4m3fn_x4
+ALU = mybir.AluOpType
+ACT = mybir.ActivationFunctionType
+
+P = 128
+K, T, S, G, H, W, C = 512, 1024, 256, 2048, 512, 128, 512
+HALF = 256
+SHARED_AT = {
+    "pab1": 0, "code_b": 0, "z0_0": 0, "z0_1": 512, "z1_0": 1024, "z1_1": 1536, "picked_c": 2048,
+    "code_a0": 3072, "picked_b": 3072,
+    "pab3": 4096, "code_c": 4096,
+}
+FLOPS = 2 * K * H * S * 3 + 2 * K * C * S
+
+
+def tile_picked_mtthzceordcpsw_none_p_kernel(
+    tc, x_words, x_scales, d_words, d_scales, sl, th, gs,
+    offs, k1, two, k2, hz, k3, n1, n2, n3, n4, n5, cand, n6, n7, n8, n9, n10, out,
+):
+    nc = tc.nc
+    with ExitStack() as ctx:
+        lists = ctx.enter_context(tc.tile_pool(name="lists", bufs=1))
+        keep = ctx.enter_context(tc.tile_pool(name="keep", bufs=1))
+        shared = ctx.enter_context(tc.tile_pool(name="shared", bufs=1))
+        psum = ctx.enter_context(tc.psum_pool(name="psum", bufs=1))
+
+        def sb(name, cols, dtype):
+            if name in SHARED_AT:
+                return shared.tile([P] + list(cols), dtype, name=name, tag=name, align_bytes=64, offset=SHARED_AT[name])
+            return keep.tile([P] + list(cols), dtype, name=name, tag=name, align_bytes=64)
+
+        def load_list(name, ap):
+            t = lists.tile(list(ap.shape), U16, name=name)
+            nc.sync.dma_start(t[:], ap)
+            return t
+
+        def entries(lst, first, count):
+            return lst[:, first // 16 : (first + count) // 16]
+
+        def zero_bytes(t):
+            nc.vector.memset(t[:].bitcast(U32), 0)
+
+        def place_scale_rows(queue, plane, picked):
+            for r in range(4):
+                queue.dma_start(out=plane[r:P:32, :].bitcast(I32), in_=picked[8 * r : P : 32, :].bitcast(I32))
+
+        xs = sb("xs", [T], U8)
+        ds = sb("ds", [G], U8)
+        zero_bytes(xs)
+        zero_bytes(ds)
+        nc.sync.dma_start(out=xs[0:P:8, :].bitcast(I32), in_=x_scales[0].bitcast(I32))
+        l_hz = load_list("l_hz", hz)
+        nc.sync.dma_start(out=ds[0:P:8, :].bitcast(I32), in_=d_scales[0].bitcast(I32))
+        l_k = [load_list("l_k1", k1), load_list("l_k2", k2), load_list("l_k3", k3)]
+        l_x = [load_list("l_offs", offs), load_list("l_two", two), l_hz]
+        xw = sb("xw", [T], U32)
+        dw = sb("dw", [G], U32)
+        nc.sync.dma_start(out=xw[:].bitcast(I32), in_=x_words[0].rearrange("p n t -> p (n t)").bitcast(I32))
+        nc.sync.dma_start(out=dw[:].bitcast(I32), in_=d_words[0].rearrange("p n t -> p (n t)").bitcast(I32))
+        l_n1, l_n2, l_n3, l_n4, l_n5 = [load_list("l_n%d" % (i + 1), a) for i, a in enumerate((n1, n2, n3, n4, n5))]
+        l_cand = load_list("l_cand", cand)
+        l_n6, l_n7, l_n8, l_n9, l_n10 = [load_list("l_n%d" % (i + 6), a) for i, a in enumerate((n6, n7, n8, n9, n10))]
+
+        plane_a = sb("plane_a", [3 * S + 3 * HALF], U8)
+        plane_b = sb("plane_b", [3 * HALF], U8)
+        plane_c = sb("plane_c", [C], U8)
+        for t in (plane_a, plane_b, plane_c):
+            zero_bytes(t)
+
+        ident = sb("ident", [P], F32)
+        make_identity(nc, ident[:])
+        rowvals = []
+        with nc.allow_non_contiguous_dma(reason="one float32 value a row"):
+            for name, ap in (("sl_t", sl), ("th_t", th), ("gs_t", gs)):
+                t = sb(name, [4], F32)
+                nc.gpsimd.dma_start(out=t[:], in_=ap.rearrange("(a p) o -> p (a o)", p=P))
+                rowvals.append(t)
+        sl_t, th_t, gs_t = rowvals
+
+        picked_a = sb("picked_a", [3 * S + 3 * HALF], U8)
+        nc.vector.tensor_copy(picked_a[:, 2 * S : 3 * S], xs[:].indirect(l_x[2][:]))
+        for m in range(3):
+            c0 = 3 * S + m * HALF
+            nc.vector.tensor_copy(picked_a[:, c0 : c0 + HALF], ds[:].indirect(entries(l_k[m], 0, HALF)))
+        for m in range(2):
+            nc.vector.tensor_copy(picked_a[:, m * S : (m + 1) * S], xs[:].indirect(l_x[m][:]))
+        place_scale_rows(nc.scalar, plane_a, picked_a)
+
+        xq = sb("xq", [3 * S], U32)
+        for m in range(3):
+            nc.vector.tensor_copy(xq[:, m * S : (m + 1) * S], xw[:].indirect(l_x[m][:]))
+        code_a = []
+        for m in range(3):
+            t = sb("code_a%d" % m, [HALF], U32)
+            nc.vector.tensor_copy(t[:], dw[:].indirect(entries(l_k[m], 0, HALF)))
+            code_a.append(t[:])
+
+        nbias = sb("nbias", [4], F32)
+        slth = sb("slth", [4], F32)
+        nc.gpsimd.tensor_tensor(slth[:], sl_t[:], th_t[:], ALU.mult)
+        nc.gpsimd.tensor_scalar(nbias[:], slth[:], -1.0, 0.0, ALU.mult, ALU.add)
+
+        def first_product(pair, codes, planes):
+            banks = [psum.tile([P, S], F32, name="acc%d" % a, tag="acc%d" % a) for a in pair]
+            for m in range(3):
+                for i in range(2):
+                    nc.tensor.matmul_mx(
+                        banks[i][:],
+                        lhsT=codes[m][:, i * P : (i + 1) * P].bitcast(FP8X4),
+                        lhsT_scale=planes[m][:, i * P : (i + 1) * P],
+                        rhs=xq[:, m * S : (m + 1) * S].bitcast(FP8X4),
+                        rhs_scale=plane_a[:, m * S : (m + 1) * S],
+                        start=(m == 0),
+                        stop=(m == 2),
+                    )
+            return banks
+
+        def to_sbuf(name, bank, on_scalar):
+            t = sb(name, [S], F32)
+            if on_scalar:
+                nc.scalar.activation(t[:], bank[:], ACT.Copy, scale=0.0625)
+            else:
+                nc.vector.tensor_scalar(t[:], bank[:], 0.0625, None, ALU.mult)
+            return t
+
+        def fetch_pairs(name, window, la, lb):
+            t = sb(name, [2 * W], F32)
+            nc.scalar.activation(t[:, W:], window[:].indirect(lb[:]), ACT.Copy)
+            nc.scalar.activation(t[:, :W], window[:].indirect(la[:]), ACT.Copy)
+            return t
+
+        def scatter(window, lst, values):
+            nc.scalar.activation(window[:].indirect(lst[:]), values, ACT.Copy)
+
+        z_pairs = [sb("z_pairs%d" % j, [2, P, 2], BF16) for j in range(2)]
+
+        def sort_pair(pair, fetch_h):
+            sorted_vals = []
+            for a in pair:
+                h = fetch_h(a)
+                pab = fetch_pairs("pab%d" % a, h, l_n1, l_n2)
+                rab = sb("rab%d" % a, [2 * W], F32)
+                nc.vector.tensor_tensor(rab[:, :W], pab[:, :W], pab[:, W:], ALU.max)
+                nc.vector.tensor_tensor(rab[:, W:], pab[:, :W], pab[:, W:], ALU.min)
+                sorted_vals.append(rab)
+            return sorted_vals
+
+        def gate_pair(pair, sorted_vals):
+            ubs = [sb("ub%d" % a, [S], F32) for a in pair]
+            for ub, rab in zip(ubs, sorted_vals):
+                scatter(ub, l_n3, rab[:, :W])
+            for ub, rab in zip(ubs, sorted_vals):
+                scatter(ub, l_n4, rab[:, W:])
+            for j in range(2):
+                cols = slice(j * P, (j + 1) * P)
+                for a, ub in zip(pair, ubs):
+                    sg = sb("sg%d_%d" % (a, j), [P], F32)
+                    nc.scalar.activation(
+                        sg[:], ub[:].indirect(entries(l_n5, j * P, P)), ACT.Sigmoid,
+                        bias=nbias[:, a : a + 1], scale=sl_t[:, a : a + 1],
+                    )
+                    z = sb("z%d_%d" % (a, j), [P], F32)
+                    nc.vector.scalar_tensor_tensor(z[:], sg[:], gs_t[:, a : a + 1], ub[:, cols], ALU.mult, ALU.mult)
+                    zt = psum.tile([P, P], F32, name="zt%d_%d" % (a, j), tag="zt%d" % (a % 2))
+                    nc.tensor.transpose(zt[:], z[:], ident[:])
+                    move = nc.scalar.copy if (a, j) == (3, 1) else nc.vector.tensor_copy
+                    move(
+                        z_pairs[j][:, :, 32 * a : 32 * (a + 1), :],
+                        zt[:].rearrange("j (p u e) -> j u p e", u=2, e=2),
+                    )
+
+        banks = first_product((0, 1), code_a, [plane_a[:, 3 * S + m * HALF : 3 * S + (m + 1) * HALF] for m in range(3)])
+
+        picked_b = sb("picked_b", [3 * HALF], U8)
+        for m in range(3):
+            nc.vector.tensor_copy(picked_b[:, m * HALF : (m + 1) * HALF], ds[:].indirect(entries(l_k[m], HALF, HALF)))
+        place_scale_rows(nc.sync, plane_b, picked_b)
+
+        sorted_vals = sort_pair((0, 1), lambda a: to_sbuf("h%d" % a, banks[a], True))
+
+        code_b = sb("code_b", [3 * HALF], U32)
+        for m in range(3):
+            nc.vector.tensor_copy(code_b[:, m * HALF : (m + 1) * HALF], dw[:].indirect(entries(l_k[m], HALF, HALF)))
+        banks = first_product(
+            (2, 3),
+            [code_b[:, m * HALF : (m + 1) * HALF] for m in range(3)],
+            [plane_b[:, m * HALF : (m + 1) * HALF] for m in range(3)],
+        )
+
+        late_h = [to_sbuf("h%d" % (2 + i), banks[i], False) for i in range(2)]
+        picked_c = sb("picked_c", [C], U8)
+        nc.vector.tensor_copy(picked_c[:], xs[:].indirect(l_cand[:]))
+        place_scale_rows(nc.sync, plane_c, picked_c)
+
+        gate_pair((0, 1), sorted_vals)
+        sorted_vals = sort_pair((2, 3), lambda a: late_h[a - 2])
+        code_c = sb("code_c", [C], U32)
+        nc.vector.tensor_copy(code_c[:], xw[:].indirect(l_cand[:]))
+
+        gate_pair((2, 3), sorted_vals)
+
+        s_banks = [psum.tile([P, S], F32, name="sacc%d" % c, tag="acc%d" % c) for c in range(4)]
+        for j in range(2):
+            zk = psum.tile([P, 2, P], F32, name="zk%d" % j, tag="zk%d" % j)
+            for u in range(2):
+                nc.tensor.transpose(zk[:, u, :], z_pairs[j][:, u, :, :].rearrange("j p e -> j (p e)").bitcast(F32), ident[:])
+            zq = sb("zq%d" % j, [4 * P], BF16)
+            move = nc.scalar.copy if j == 1 else nc.vector.tensor_copy
+            move(zq[:].bitcast(F32).rearrange("p (j u) -> p j u", u=2), zk[:].rearrange("p u j -> p j u"))
+            z_codes = sb("z_codes%d" % j, [P], U32)
+            z_scales = sb("z_scales%d" % j, [P], U8)
+            nc.vector.quantize_mx(z_codes[:].bitcast(FP8X4), z_scales[:], zq[:])
+            for c in range(4):
+                nc.tensor.matmul_mx(
+                    s_banks[c][:, j * P : (j + 1) * P],
+                    lhsT=code_c[:, c * P : (c + 1) * P].bitcast(FP8X4),
+                    lhsT_scale=plane_c[:, c * P : (c + 1) * P],
+                    rhs=z_codes[:].bitcast(FP8X4),
+                    rhs_scale=z_scales[:],
+                    start=True,
+                    stop=True,
+                )
+
+        for c in range(4):
+            s = to_sbuf("s%d" % c, s_banks[c], c == 0)
+            pab = fetch_pairs("pab2_%d" % c, s, l_n6, l_n7)
+            rb = sb("rb2_%d" % c, [W], F32)
+            nc.vector.tensor_tensor(rb[:], pab[:, :W], pab[:, W:], ALU.max)
+            ub = sb("ub2_%d" % c, [S], F32)
+            scatter(ub, l_n8, pab[:, W:])
+            sn = sb("sn%d" % c, [S], F32)
+            for j in range(2):
+                nc.scalar.activation(sn[:, j * P : (j + 1) * P], s[:].indirect(entries(l_n10, j * P, P)), ACT.Copy)
+            scatter(ub, l_n9, rb[:])
+            res = sb("res%d" % c, [S], F32)
+            nc.vector.tensor_tensor(res[:], ub[:], sn[:], ALU.subtract)
+            nc.sync.dma_start(out=out[c * P : (c + 1) * P, :], in_=res[:])

@@ -72,6 +72,10 @@ def tile_picked_mtthzceordcpsw_none_p_kernel(
         l_cand = load_list("l_cand", cand)
         l_n6, l_n7, l_n8, l_n9, l_n10 = [load_list("l_n%d" % (i + 6), a) for i, a in enumerate((n6, n7, n8, n9, n10))]
 
+        warm = sb("warm", [1], F32)
+        warm_out = sb("warm_out", [1], F32)
+        nc.vector.memset(warm[:], 0.0)
+        nc.scalar.activation(warm_out[:], warm[:], ACT.Sigmoid)
         plane_a = sb("plane_a", [3 * S + 3 * HALF], U8)
         plane_b = sb("plane_b", [3 * HALF], U8)
         plane_c = sb("plane_c", [C], U8)

@@ -17,10 +17,12 @@ P = 128
 K, T, S, G, H, W, C = 512, 1024, 256, 2048, 512, 128, 512
 HALF = 256
 SHARED_AT = {
-    "pab1": 0, "code_b": 0, "z0_0": 0, "z0_1": 512, "z1_0": 1024, "z1_1": 1536, "picked_c": 2048,
+    "pab1": 0, "code_b": 0, "z0_0": 0, "z0_1": 512, "picked_c": 2048,
     "code_a0": 3072, "picked_b": 3072,
-    "pab3": 4096, "code_c": 4096,
+    "code_c": 4096, "pab3": 5888, "z1_0": 6144, "z1_1": 6656,
 }
+SPARE = 16
+LAST = 64
 FLOPS = 2 * K * H * S * 3 + 2 * K * C * S
 
 
@@ -59,9 +61,9 @@ def tile_picked_mtthzceordcpsw_none_p_kernel(
         ds = sb("ds", [G], U8)
         zero_bytes(xs)
         zero_bytes(ds)
-        nc.sync.dma_start(out=xs[0:P:8, :].bitcast(I32), in_=x_scales[0].bitcast(I32))
+        nc.scalar.dma_start(out=xs[0:P:8, :].bitcast(I32), in_=x_scales[0].bitcast(I32))
         l_hz = load_list("l_hz", hz)
-        nc.sync.dma_start(out=ds[0:P:8, :].bitcast(I32), in_=d_scales[0].bitcast(I32))
+        nc.scalar.dma_start(out=ds[0:P:8, :].bitcast(I32), in_=d_scales[0].bitcast(I32))
         l_k = [load_list("l_k1", k1), load_list("l_k2", k2), load_list("l_k3", k3)]
         l_x = [load_list("l_offs", offs), load_list("l_two", two), l_hz]
         xw = sb("xw", [T], U32)
@@ -81,6 +83,13 @@ def tile_picked_mtthzceordcpsw_none_p_kernel(
         plane_c = sb("plane_c", [C], U8)
         for t in (plane_a, plane_b, plane_c):
             zero_bytes(t)
+
+        ub_tiles = [sb("ub%d" % a, [2 * S if a < 2 else S], F32) for a in range(4)]
+        s_tiles = [sb("s%d" % c, [S + SPARE], F32) for c in range(4)]
+        for a in range(2):
+            nc.vector.memset(ub_tiles[a][:, S:], 0.0)
+        for c in range(4):
+            nc.vector.memset(s_tiles[c][:, S:], 0.0)
 
         ident = sb("ident", [P], F32)
         make_identity(nc, ident[:])
@@ -160,29 +169,36 @@ def tile_picked_mtthzceordcpsw_none_p_kernel(
                 sorted_vals.append(rab)
             return sorted_vals
 
-        def gate_pair(pair, sorted_vals):
-            ubs = [sb("ub%d" % a, [S], F32) for a in pair]
-            for ub, rab in zip(ubs, sorted_vals):
-                scatter(ub, l_n3, rab[:, :W])
-            for ub, rab in zip(ubs, sorted_vals):
-                scatter(ub, l_n4, rab[:, W:])
-            for j in range(2):
-                cols = slice(j * P, (j + 1) * P)
-                for a, ub in zip(pair, ubs):
-                    sg = sb("sg%d_%d" % (a, j), [P], F32)
-                    nc.scalar.activation(
-                        sg[:], ub[:].indirect(entries(l_n5, j * P, P)), ACT.Sigmoid,
-                        bias=nbias[:, a : a + 1], scale=sl_t[:, a : a + 1],
-                    )
-                    z = sb("z%d_%d" % (a, j), [P], F32)
-                    nc.vector.scalar_tensor_tensor(z[:], sg[:], gs_t[:, a : a + 1], ub[:, cols], ALU.mult, ALU.mult)
-                    zt = psum.tile([P, P], F32, name="zt%d_%d" % (a, j), tag="zt%d" % (a % 2))
-                    nc.tensor.transpose(zt[:], z[:], ident[:])
-                    move = nc.scalar.copy if (a, j) == (3, 1) else nc.vector.tensor_copy
-                    move(
-                        z_pairs[j][:, :, 32 * a : 32 * (a + 1), :],
-                        zt[:].rearrange("j (p u e) -> j u p e", u=2, e=2),
-                    )
+        def gate(a, first, count):
+            sg = sb("sg%d_%d" % (a, first), [count], F32)
+            nc.scalar.activation(
+                sg[:], ub_tiles[a][:].indirect(entries(l_n5, first, count)), ACT.Sigmoid,
+                bias=nbias[:, a : a + 1], scale=sl_t[:, a : a + 1],
+            )
+            return sg
+
+        def turned(name, src, tag):
+            bank = psum.tile([P, P], F32, name=name, tag=tag)
+            nc.tensor.transpose(bank[:], src, ident[:])
+            return bank
+
+        def pairs_of(a, j):
+            return z_pairs[j][:, :, 32 * a : 32 * (a + 1), :]
+
+        def dealt(ap):
+            return ap.rearrange("j (p u e) -> j u p e", u=2, e=2)
+
+        def z_block(a, j, sg, move, bank_tag):
+            z = sb("z%d_%d" % (a, j), [P], F32)
+            nc.vector.scalar_tensor_tensor(z[:], sg, gs_t[:, a : a + 1], ub_tiles[a][:, j * P : (j + 1) * P], ALU.mult, ALU.mult)
+            zt = turned("zt%d_%d" % (a, j), z[:], bank_tag)
+            move(pairs_of(a, j), dealt(zt[:]))
+
+        def put_back(pair, sorted_vals):
+            for a, rab in zip(pair, sorted_vals):
+                scatter(ub_tiles[a], l_n3, rab[:, :W])
+            for a, rab in zip(pair, sorted_vals):
+                scatter(ub_tiles[a], l_n4, rab[:, W:])
 
         banks = first_product((0, 1), code_a, [plane_a[:, 3 * S + m * HALF : 3 * S + (m + 1) * HALF] for m in range(3)])
 
@@ -191,7 +207,8 @@ def tile_picked_mtthzceordcpsw_none_p_kernel(
             nc.vector.tensor_copy(picked_b[:, m * HALF : (m + 1) * HALF], ds[:].indirect(entries(l_k[m], HALF, HALF)))
         place_scale_rows(nc.sync, plane_b, picked_b)
 
-        sorted_vals = sort_pair((0, 1), lambda a: to_sbuf("h%d" % a, banks[a], True))
+        early_h = [to_sbuf("h%d" % a, banks[a], True) for a in range(2)]
+        sorted_vals = sort_pair((0, 1), lambda a: early_h[a])
 
         code_b = sb("code_b", [3 * HALF], U32)
         for m in range(3):
@@ -207,46 +224,76 @@ def tile_picked_mtthzceordcpsw_none_p_kernel(
         nc.vector.tensor_copy(picked_c[:], xs[:].indirect(l_cand[:]))
         place_scale_rows(nc.sync, plane_c, picked_c)
 
-        gate_pair((0, 1), sorted_vals)
+        put_back((0, 1), sorted_vals)
+        early_sg = [gate(a, 0, S) for a in range(2)]
+
+        def early_z(a):
+            for j in range(2):
+                z_block(a, j, early_sg[a][:, j * P : (j + 1) * P], nc.vector.tensor_copy, "zt%d" % j)
+
+        early_z(0)
         sorted_vals = sort_pair((2, 3), lambda a: late_h[a - 2])
+        early_z(1)
         code_c = sb("code_c", [C], U32)
         nc.vector.tensor_copy(code_c[:], xw[:].indirect(l_cand[:]))
 
-        gate_pair((2, 3), sorted_vals)
+        put_back((2, 3), sorted_vals)
+        gub = sb("gub", [P], F32)
+        nc.vector.tensor_scalar(gub[:], ub_tiles[3][:, P:], gs_t[:, 3:4], None, ALU.mult)
+        gub_bank = turned("gub_bank", gub[:], "zk1")
+        gub_t = sb("gub_t", [P], F32)
+        nc.vector.tensor_copy(gub_t[:], gub_bank[:])
+        for a in (2, 3):
+            z_block(a, 0, gate(a, 0, P)[:], nc.vector.tensor_copy, "zt%d" % (a - 2))
+        z_block(2, 1, gate(2, P, P)[:], nc.scalar.copy, "acc2")
+        sg_bank = turned("sg_bank", gate(3, P, P)[:], "acc1")
+        nc.vector.tensor_tensor(pairs_of(3, 1), dealt(sg_bank[:]), dealt(gub_t[:]), ALU.mult)
 
-        s_banks = [psum.tile([P, S], F32, name="sacc%d" % c, tag="acc%d" % c) for c in range(4)]
+        z_codes = sb("z_codes", [S], U32)
+        z_scales = sb("z_scales", [S], U8)
+
+        def scores(bank, c, cols):
+            nc.tensor.matmul_mx(
+                bank,
+                lhsT=code_c[:, c * P : (c + 1) * P].bitcast(FP8X4),
+                lhsT_scale=plane_c[:, c * P : (c + 1) * P],
+                rhs=z_codes[:, cols].bitcast(FP8X4),
+                rhs_scale=z_scales[:, cols],
+                start=True,
+                stop=True,
+            )
+
         for j in range(2):
+            cols = slice(j * P, (j + 1) * P)
             zk = psum.tile([P, 2, P], F32, name="zk%d" % j, tag="zk%d" % j)
             for u in range(2):
                 nc.tensor.transpose(zk[:, u, :], z_pairs[j][:, u, :, :].rearrange("j p e -> j (p e)").bitcast(F32), ident[:])
             zq = sb("zq%d" % j, [4 * P], BF16)
             move = nc.scalar.copy if j == 1 else nc.vector.tensor_copy
             move(zq[:].bitcast(F32).rearrange("p (j u) -> p j u", u=2), zk[:].rearrange("p u j -> p j u"))
-            z_codes = sb("z_codes%d" % j, [P], U32)
-            z_scales = sb("z_scales%d" % j, [P], U8)
-            nc.vector.quantize_mx(z_codes[:].bitcast(FP8X4), z_scales[:], zq[:])
-            for c in range(4):
-                nc.tensor.matmul_mx(
-                    s_banks[c][:, j * P : (j + 1) * P],
-                    lhsT=code_c[:, c * P : (c + 1) * P].bitcast(FP8X4),
-                    lhsT_scale=plane_c[:, c * P : (c + 1) * P],
-                    rhs=z_codes[:].bitcast(FP8X4),
-                    rhs_scale=z_scales[:],
-                    start=True,
-                    stop=True,
-                )
+            nc.vector.quantize_mx(z_codes[:, cols].bitcast(FP8X4), z_scales[:, cols], zq[:])
+            half = psum.tile([P, P], F32, name="s0_half%d" % j, tag=("zk0", "acc0")[j])
+            scores(half[:], 0, cols)
+            nc.scalar.activation(s_tiles[0][:, cols], half[:], ACT.Copy, scale=0.0625)
+
+        for c in range(1, 4):
+            bank = psum.tile([P, S], F32, name="sacc%d" % c, tag="acc%d" % c)
+            scores(bank[:], c, slice(0, S))
+            nc.vector.tensor_scalar(s_tiles[c][:, :S], bank[:], 0.0625, None, ALU.mult)
 
         for c in range(4):
-            s = to_sbuf("s%d" % c, s_banks[c], c == 0)
+            s = s_tiles[c]
             pab = fetch_pairs("pab2_%d" % c, s, l_n6, l_n7)
             rb = sb("rb2_%d" % c, [W], F32)
             nc.vector.tensor_tensor(rb[:], pab[:, :W], pab[:, W:], ALU.max)
             ub = sb("ub2_%d" % c, [S], F32)
             scatter(ub, l_n8, pab[:, W:])
-            sn = sb("sn%d" % c, [S], F32)
-            for j in range(2):
-                nc.scalar.activation(sn[:, j * P : (j + 1) * P], s[:].indirect(entries(l_n10, j * P, P)), ACT.Copy)
-            scatter(ub, l_n9, rb[:])
-            res = sb("res%d" % c, [S], F32)
-            nc.vector.tensor_tensor(res[:], ub[:], sn[:], ALU.subtract)
-            nc.sync.dma_start(out=out[c * P : (c + 1) * P, :], in_=res[:])
+            pieces = [(0, S)] if c < 3 else [(0, S - LAST), (S - LAST, LAST)]
+            for i, (first, count) in enumerate(pieces):
+                sn = sb("sn%d_%d" % (c, i), [count], F32)
+                nc.scalar.activation(sn[:], s[:].indirect(entries(l_n10, first, count)), ACT.Copy)
+                if i == 0:
+                    scatter(ub, l_n9, rb[:])
+                res = sb("res%d_%d" % (c, i), [count], F32)
+                nc.vector.tensor_tensor(res[:], ub[:, first : first + count], sn[:], ALU.subtract)
+                nc.sync.dma_start(out=out[c * P : (c + 1) * P, first : first + count], in_=res[:])

@@ -15,15 +15,18 @@ ACT = mybir.ActivationFunctionType
 
 P = 128
 K, T, S, G, H, W, C = 512, 1024, 256, 2048, 512, 128, 512
-HALF = 256
-SHARED_AT = {
-    "pab1": 0, "code_b": 0, "z0_0": 0, "z0_1": 512, "picked_c": 2048,
-    "code_a0": 3072, "picked_b": 3072,
-    "code_c": 4096, "pab3": 5888, "z1_0": 6144, "z1_1": 6656,
-}
+TILES = 4
+HALF = H // 2
+SIXTEENTH = 0.0625
 SPARE = 16
 LAST = 64
 FLOPS = 2 * K * H * S * 3 + 2 * K * C * S
+
+SHARED_AT = {
+    "pairs_h1": 0, "codes_late": 0, "z0_0": 0, "z0_1": 512, "picked_cand": 2048,
+    "codes_early0": 3072, "picked_late": 3072,
+    "pairs_h3": 5888, "codes_cand": 4096, "z1_0": 6144, "z1_1": 6656,
+}
 
 
 def tile_picked_mtthzceordcpsw_none_p_kernel(
@@ -39,8 +42,14 @@ def tile_picked_mtthzceordcpsw_none_p_kernel(
 
         def sb(name, cols, dtype):
             if name in SHARED_AT:
-                return shared.tile([P] + list(cols), dtype, name=name, tag=name, align_bytes=64, offset=SHARED_AT[name])
-            return keep.tile([P] + list(cols), dtype, name=name, tag=name, align_bytes=64)
+                return shared.tile([P] + cols, dtype, name=name, tag=name, align_bytes=64, offset=SHARED_AT[name])
+            return keep.tile([P] + cols, dtype, name=name, tag=name, align_bytes=64)
+
+        def bank(name, cols, number):
+            return psum.tile([P] + cols, F32, name=name, tag="bank%d" % number)
+
+        def block(i, width=P):
+            return slice(i * width, (i + 1) * width)
 
         def load_list(name, ap):
             t = lists.tile(list(ap.shape), U16, name=name)
@@ -56,6 +65,12 @@ def tile_picked_mtthzceordcpsw_none_p_kernel(
         def place_scale_rows(queue, plane, picked):
             for r in range(4):
                 queue.dma_start(out=plane[r:P:32, :].bitcast(I32), in_=picked[8 * r : P : 32, :].bitcast(I32))
+
+        def mx_pass(acc, lhs_words, lhs_plane, rhs_words, rhs_plane, start, stop):
+            nc.tensor.matmul_mx(
+                acc, lhsT=lhs_words.bitcast(FP8X4), lhsT_scale=lhs_plane,
+                rhs=rhs_words.bitcast(FP8X4), rhs_scale=rhs_plane, start=start, stop=stop,
+            )
 
         xs = sb("xs", [T], U8)
         ds = sb("ds", [G], U8)
@@ -78,96 +93,84 @@ def tile_picked_mtthzceordcpsw_none_p_kernel(
         warm_out = sb("warm_out", [1], F32)
         nc.vector.memset(warm[:], 0.0)
         nc.scalar.activation(warm_out[:], warm[:], ACT.Sigmoid)
-        plane_a = sb("plane_a", [3 * S + 3 * HALF], U8)
-        plane_b = sb("plane_b", [3 * HALF], U8)
-        plane_c = sb("plane_c", [C], U8)
-        for t in (plane_a, plane_b, plane_c):
-            zero_bytes(t)
 
-        ub_tiles = [sb("ub%d" % a, [2 * S if a < 2 else S], F32) for a in range(4)]
-        s_tiles = [sb("s%d" % c, [S + SPARE], F32) for c in range(4)]
-        for a in range(2):
-            nc.vector.memset(ub_tiles[a][:, S:], 0.0)
-        for c in range(4):
-            nc.vector.memset(s_tiles[c][:, S:], 0.0)
+        plane_early = sb("plane_early", [3 * S + 3 * HALF], U8)
+        plane_late = sb("plane_late", [3 * HALF], U8)
+        plane_cand = sb("plane_cand", [C], U8)
+        for plane in (plane_early, plane_late, plane_cand):
+            zero_bytes(plane)
+
+        ub_tiles = [sb("ub%d" % a, [2 * S if a < TILES - 1 else S], F32) for a in range(TILES)]
+        s_tiles = [sb("s%d" % c, [S + SPARE], F32) for c in range(TILES)]
+        for t in ub_tiles[:-1] + s_tiles:
+            nc.vector.memset(t[:, S:], 0.0)
 
         ident = sb("ident", [P], F32)
         make_identity(nc, ident[:])
-        rowvals = []
+        row_values = []
         with nc.allow_non_contiguous_dma(reason="one float32 value a row"):
             for name, ap in (("sl_t", sl), ("th_t", th), ("gs_t", gs)):
-                t = sb(name, [4], F32)
+                t = sb(name, [TILES], F32)
                 nc.gpsimd.dma_start(out=t[:], in_=ap.rearrange("(a p) o -> p (a o)", p=P))
-                rowvals.append(t)
-        sl_t, th_t, gs_t = rowvals
+                row_values.append(t)
+        sl_t, th_t, gs_t = row_values
 
-        picked_a = sb("picked_a", [3 * S + 3 * HALF], U8)
-        nc.vector.tensor_copy(picked_a[:, 2 * S : 3 * S], xs[:].indirect(l_x[2][:]))
+        picked_early = sb("picked_early", [3 * S + 3 * HALF], U8)
+        nc.vector.tensor_copy(picked_early[:, block(2, S)], xs[:].indirect(l_x[2][:]))
         for m in range(3):
-            c0 = 3 * S + m * HALF
-            nc.vector.tensor_copy(picked_a[:, c0 : c0 + HALF], ds[:].indirect(entries(l_k[m], 0, HALF)))
+            nc.vector.tensor_copy(picked_early[:, block(3 + m, HALF)], ds[:].indirect(entries(l_k[m], 0, HALF)))
         for m in range(2):
-            nc.vector.tensor_copy(picked_a[:, m * S : (m + 1) * S], xs[:].indirect(l_x[m][:]))
-        place_scale_rows(nc.scalar, plane_a, picked_a)
+            nc.vector.tensor_copy(picked_early[:, block(m, S)], xs[:].indirect(l_x[m][:]))
+        place_scale_rows(nc.scalar, plane_early, picked_early)
 
-        xq = sb("xq", [3 * S], U32)
+        x_codes = sb("x_codes", [3 * S], U32)
         for m in range(3):
-            nc.vector.tensor_copy(xq[:, m * S : (m + 1) * S], xw[:].indirect(l_x[m][:]))
-        code_a = []
+            nc.vector.tensor_copy(x_codes[:, block(m, S)], xw[:].indirect(l_x[m][:]))
+        codes_early = []
         for m in range(3):
-            t = sb("code_a%d" % m, [HALF], U32)
+            t = sb("codes_early%d" % m, [HALF], U32)
             nc.vector.tensor_copy(t[:], dw[:].indirect(entries(l_k[m], 0, HALF)))
-            code_a.append(t[:])
+            codes_early.append(t[:])
 
-        nbias = sb("nbias", [4], F32)
-        slth = sb("slth", [4], F32)
-        nc.gpsimd.tensor_tensor(slth[:], sl_t[:], th_t[:], ALU.mult)
-        nc.gpsimd.tensor_scalar(nbias[:], slth[:], -1.0, 0.0, ALU.mult, ALU.add)
+        sl_th = sb("sl_th", [TILES], F32)
+        nbias = sb("nbias", [TILES], F32)
+        nc.gpsimd.tensor_tensor(sl_th[:], sl_t[:], th_t[:], ALU.mult)
+        nc.gpsimd.tensor_scalar(nbias[:], sl_th[:], -1.0, 0.0, ALU.mult, ALU.add)
 
-        def first_product(pair, codes, planes):
-            banks = [psum.tile([P, S], F32, name="acc%d" % a, tag="acc%d" % a) for a in pair]
+        def first_product(numbers, codes, planes):
+            accs = [bank("h_acc%d" % a, [S], a) for a in numbers]
             for m in range(3):
                 for i in range(2):
-                    nc.tensor.matmul_mx(
-                        banks[i][:],
-                        lhsT=codes[m][:, i * P : (i + 1) * P].bitcast(FP8X4),
-                        lhsT_scale=planes[m][:, i * P : (i + 1) * P],
-                        rhs=xq[:, m * S : (m + 1) * S].bitcast(FP8X4),
-                        rhs_scale=plane_a[:, m * S : (m + 1) * S],
-                        start=(m == 0),
-                        stop=(m == 2),
+                    mx_pass(
+                        accs[i][:], codes[m][:, block(i)], planes[m][:, block(i)],
+                        x_codes[:, block(m, S)], plane_early[:, block(m, S)], m == 0, m == 2,
                     )
-            return banks
+            return accs
 
-        def to_sbuf(name, bank, on_scalar):
-            t = sb(name, [S], F32)
-            if on_scalar:
-                nc.scalar.activation(t[:], bank[:], ACT.Copy, scale=0.0625)
-            else:
-                nc.vector.tensor_scalar(t[:], bank[:], 0.0625, None, ALU.mult)
-            return t
-
-        def fetch_pairs(name, window, la, lb):
+        def fetch_pairs(name, window, first_list, second_list):
             t = sb(name, [2 * W], F32)
-            nc.scalar.activation(t[:, W:], window[:].indirect(lb[:]), ACT.Copy)
-            nc.scalar.activation(t[:, :W], window[:].indirect(la[:]), ACT.Copy)
+            nc.scalar.activation(t[:, W:], window[:].indirect(second_list[:]), ACT.Copy)
+            nc.scalar.activation(t[:, :W], window[:].indirect(first_list[:]), ACT.Copy)
             return t
 
         def scatter(window, lst, values):
             nc.scalar.activation(window[:].indirect(lst[:]), values, ACT.Copy)
 
-        z_pairs = [sb("z_pairs%d" % j, [2, P, 2], BF16) for j in range(2)]
-
-        def sort_pair(pair, fetch_h):
-            sorted_vals = []
-            for a in pair:
-                h = fetch_h(a)
-                pab = fetch_pairs("pab%d" % a, h, l_n1, l_n2)
-                rab = sb("rab%d" % a, [2 * W], F32)
+        def sort_pairs(numbers):
+            results = []
+            for a in numbers:
+                pab = fetch_pairs("pairs_h%d" % a, h_tiles[a], l_n1, l_n2)
+                rab = sb("ordered%d" % a, [2 * W], F32)
                 nc.vector.tensor_tensor(rab[:, :W], pab[:, :W], pab[:, W:], ALU.max)
                 nc.vector.tensor_tensor(rab[:, W:], pab[:, :W], pab[:, W:], ALU.min)
-                sorted_vals.append(rab)
-            return sorted_vals
+                results.append(rab)
+            return results
+
+        def put_back(numbers, ordered):
+            for a, rab in zip(numbers, ordered):
+                scatter(ub_tiles[a], l_n3, rab[:, :W])
+            for a, rab in zip(numbers, ordered):
+                scatter(ub_tiles[a], l_n4, rab[:, W:])
 
         def gate(a, first, count):
             sg = sb("sg%d_%d" % (a, first), [count], F32)
@@ -177,123 +180,111 @@ def tile_picked_mtthzceordcpsw_none_p_kernel(
             )
             return sg
 
-        def turned(name, src, tag):
-            bank = psum.tile([P, P], F32, name=name, tag=tag)
-            nc.tensor.transpose(bank[:], src, ident[:])
-            return bank
+        def turned(name, src, number):
+            t = bank(name, [P], number)
+            nc.tensor.transpose(t[:], src, ident[:])
+            return t
 
-        def pairs_of(a, j):
-            return z_pairs[j][:, :, 32 * a : 32 * (a + 1), :]
+        z_duos = [sb("z_duos%d" % j, [2, P, 2], BF16) for j in range(2)]
 
-        def dealt(ap):
-            return ap.rearrange("j (p u e) -> j u p e", u=2, e=2)
+        def duos_of(a, j):
+            return z_duos[j][:, :, block(a, 32), :]
 
-        def z_block(a, j, sg, move, bank_tag):
-            z = sb("z%d_%d" % (a, j), [P], F32)
-            nc.vector.scalar_tensor_tensor(z[:], sg, gs_t[:, a : a + 1], ub_tiles[a][:, j * P : (j + 1) * P], ALU.mult, ALU.mult)
-            zt = turned("zt%d_%d" % (a, j), z[:], bank_tag)
-            move(pairs_of(a, j), dealt(zt[:]))
+        def in_duo_order(rows):
+            return rows.rearrange("j (p u e) -> j u p e", u=2, e=2)
 
-        def put_back(pair, sorted_vals):
-            for a, rab in zip(pair, sorted_vals):
-                scatter(ub_tiles[a], l_n3, rab[:, :W])
-            for a, rab in zip(pair, sorted_vals):
-                scatter(ub_tiles[a], l_n4, rab[:, W:])
-
-        banks = first_product((0, 1), code_a, [plane_a[:, 3 * S + m * HALF : 3 * S + (m + 1) * HALF] for m in range(3)])
-
-        picked_b = sb("picked_b", [3 * HALF], U8)
-        for m in range(3):
-            nc.vector.tensor_copy(picked_b[:, m * HALF : (m + 1) * HALF], ds[:].indirect(entries(l_k[m], HALF, HALF)))
-        place_scale_rows(nc.sync, plane_b, picked_b)
-
-        early_h = [to_sbuf("h%d" % a, banks[a], True) for a in range(2)]
-        sorted_vals = sort_pair((0, 1), lambda a: early_h[a])
-
-        code_b = sb("code_b", [3 * HALF], U32)
-        for m in range(3):
-            nc.vector.tensor_copy(code_b[:, m * HALF : (m + 1) * HALF], dw[:].indirect(entries(l_k[m], HALF, HALF)))
-        banks = first_product(
-            (2, 3),
-            [code_b[:, m * HALF : (m + 1) * HALF] for m in range(3)],
-            [plane_b[:, m * HALF : (m + 1) * HALF] for m in range(3)],
-        )
-
-        late_h = [to_sbuf("h%d" % (2 + i), banks[i], False) for i in range(2)]
-        picked_c = sb("picked_c", [C], U8)
-        nc.vector.tensor_copy(picked_c[:], xs[:].indirect(l_cand[:]))
-        place_scale_rows(nc.sync, plane_c, picked_c)
-
-        put_back((0, 1), sorted_vals)
-        early_sg = [gate(a, 0, S) for a in range(2)]
-
-        def early_z(a):
+        def make_z(a, sg, round_copy):
             for j in range(2):
-                z_block(a, j, early_sg[a][:, j * P : (j + 1) * P], nc.vector.tensor_copy, "zt%d" % j)
+                z = sb("z%d_%d" % (a, j), [P], F32)
+                nc.vector.scalar_tensor_tensor(
+                    z[:], sg[:, block(j)], gs_t[:, a : a + 1], ub_tiles[a][:, block(j)], ALU.mult, ALU.mult
+                )
+                z_turned = turned("z_turned%d_%d" % (a, j), z[:], 4 + j)
+                round_copy(duos_of(a, j), in_duo_order(z_turned[:]))
 
-        early_z(0)
-        sorted_vals = sort_pair((2, 3), lambda a: late_h[a - 2])
-        early_z(1)
-        code_c = sb("code_c", [C], U32)
-        nc.vector.tensor_copy(code_c[:], xw[:].indirect(l_cand[:]))
+        accs_early = first_product((0, 1), codes_early, [plane_early[:, block(3 + m, HALF)] for m in range(3)])
 
-        put_back((2, 3), sorted_vals)
-        gub = sb("gub", [P], F32)
-        nc.vector.tensor_scalar(gub[:], ub_tiles[3][:, P:], gs_t[:, 3:4], None, ALU.mult)
-        gub_bank = turned("gub_bank", gub[:], "zk1")
-        gub_t = sb("gub_t", [P], F32)
-        nc.vector.tensor_copy(gub_t[:], gub_bank[:])
-        for a in (2, 3):
-            z_block(a, 0, gate(a, 0, P)[:], nc.vector.tensor_copy, "zt%d" % (a - 2))
-        z_block(2, 1, gate(2, P, P)[:], nc.scalar.copy, "acc2")
-        sg_bank = turned("sg_bank", gate(3, P, P)[:], "acc1")
-        nc.vector.tensor_tensor(pairs_of(3, 1), dealt(sg_bank[:]), dealt(gub_t[:]), ALU.mult)
+        picked_late = sb("picked_late", [3 * HALF], U8)
+        for m in range(3):
+            nc.vector.tensor_copy(picked_late[:, block(m, HALF)], ds[:].indirect(entries(l_k[m], HALF, HALF)))
+        place_scale_rows(nc.sync, plane_late, picked_late)
 
-        z_codes = sb("z_codes", [S], U32)
-        z_scales = sb("z_scales", [S], U8)
+        h_tiles = [sb("h%d" % a, [S], F32) for a in range(TILES)]
+        for a in range(2):
+            nc.scalar.activation(h_tiles[a][:], accs_early[a][:], ACT.Copy, scale=SIXTEENTH)
+        ordered_early = sort_pairs((0, 1))
 
-        def scores(bank, c, cols):
-            nc.tensor.matmul_mx(
-                bank,
-                lhsT=code_c[:, c * P : (c + 1) * P].bitcast(FP8X4),
-                lhsT_scale=plane_c[:, c * P : (c + 1) * P],
-                rhs=z_codes[:, cols].bitcast(FP8X4),
-                rhs_scale=z_scales[:, cols],
-                start=True,
-                stop=True,
+        codes_late = sb("codes_late", [3 * HALF], U32)
+        for m in range(3):
+            nc.vector.tensor_copy(codes_late[:, block(m, HALF)], dw[:].indirect(entries(l_k[m], HALF, HALF)))
+        accs_late = first_product(
+            (2, 3), [codes_late[:, block(m, HALF)] for m in range(3)], [plane_late[:, block(m, HALF)] for m in range(3)]
+        )
+        for i in range(2):
+            nc.vector.tensor_scalar(h_tiles[2 + i][:], accs_late[i][:], SIXTEENTH, None, ALU.mult)
+        picked_cand = sb("picked_cand", [C], U8)
+        nc.vector.tensor_copy(picked_cand[:], xs[:].indirect(l_cand[:]))
+        place_scale_rows(nc.sync, plane_cand, picked_cand)
+
+        put_back((0, 1), ordered_early)
+        early_sg = [gate(a, 0, S) for a in range(2)]
+        make_z(0, early_sg[0], nc.vector.tensor_copy)
+        ordered_late = sort_pairs((2, 3))
+        make_z(1, early_sg[1], nc.vector.tensor_copy)
+        codes_cand = sb("codes_cand", [C], U32)
+        nc.vector.tensor_copy(codes_cand[:], xw[:].indirect(l_cand[:]))
+
+        put_back((2, 3), ordered_late)
+        weighted = sb("weighted", [S], F32)
+        nc.vector.tensor_scalar(weighted[:], ub_tiles[3][:], gs_t[:, 3:4], None, ALU.mult)
+        weighted_turned = []
+        for j in range(2):
+            turned_bank = turned("weighted_bank%d" % j, weighted[:, block(j)], 6 + j)
+            t = sb("weighted_turned%d" % j, [P], F32)
+            nc.vector.tensor_copy(t[:], turned_bank[:])
+            weighted_turned.append(t)
+        make_z(2, gate(2, 0, S), nc.scalar.copy)
+        for j in range(2):
+            sg_turned = turned("sg_turned%d" % j, gate(3, j * P, P)[:], 1 + j)
+            nc.vector.tensor_tensor(
+                duos_of(3, j), in_duo_order(sg_turned[:]), in_duo_order(weighted_turned[j][:]), ALU.mult
             )
 
+        z_codes = sb("z_codes", [S], U32)
+        z_plane = sb("z_plane", [S], U8)
+
+        def scores(acc, c, cols):
+            mx_pass(acc, codes_cand[:, block(c)], plane_cand[:, block(c)], z_codes[:, cols], z_plane[:, cols], True, True)
+
         for j in range(2):
-            cols = slice(j * P, (j + 1) * P)
-            zk = psum.tile([P, 2, P], F32, name="zk%d" % j, tag="zk%d" % j)
+            z_back = bank("z_back%d" % j, [2, P], 6 + j)
             for u in range(2):
-                nc.tensor.transpose(zk[:, u, :], z_pairs[j][:, u, :, :].rearrange("j p e -> j (p e)").bitcast(F32), ident[:])
-            zq = sb("zq%d" % j, [4 * P], BF16)
-            move = nc.scalar.copy if j == 1 else nc.vector.tensor_copy
-            move(zq[:].bitcast(F32).rearrange("p (j u) -> p j u", u=2), zk[:].rearrange("p u j -> p j u"))
-            nc.vector.quantize_mx(z_codes[:, cols].bitcast(FP8X4), z_scales[:, cols], zq[:])
-            half = psum.tile([P, P], F32, name="s0_half%d" % j, tag=("zk0", "acc0")[j])
-            scores(half[:], 0, cols)
-            nc.scalar.activation(s_tiles[0][:, cols], half[:], ACT.Copy, scale=0.0625)
+                duos = z_duos[j][:, u, :, :].rearrange("j p e -> j (p e)").bitcast(F32)
+                nc.tensor.transpose(z_back[:, u, :], duos, ident[:])
+            z_rows = sb("z_rows%d" % j, [4 * P], BF16)
+            nc.scalar.copy(z_rows[:].bitcast(F32).rearrange("p (j u) -> p j u", u=2), z_back[:].rearrange("p u j -> p j u"))
+            nc.vector.quantize_mx(z_codes[:, block(j)].bitcast(FP8X4), z_plane[:, block(j)], z_rows[:])
+            half_acc = bank("s0_acc%d" % j, [P], (6, 0)[j])
+            scores(half_acc[:], 0, block(j))
+            nc.scalar.activation(s_tiles[0][:, block(j)], half_acc[:], ACT.Copy, scale=SIXTEENTH)
 
-        for c in range(1, 4):
-            bank = psum.tile([P, S], F32, name="sacc%d" % c, tag="acc%d" % c)
-            scores(bank[:], c, slice(0, S))
-            nc.vector.tensor_scalar(s_tiles[c][:, :S], bank[:], 0.0625, None, ALU.mult)
+        for c in range(1, TILES):
+            acc = bank("s_acc%d" % c, [S], c)
+            scores(acc[:], c, slice(0, S))
+            nc.vector.tensor_scalar(s_tiles[c][:, :S], acc[:], SIXTEENTH, None, ALU.mult)
 
-        for c in range(4):
-            s = s_tiles[c]
-            pab = fetch_pairs("pab2_%d" % c, s, l_n6, l_n7)
-            rb = sb("rb2_%d" % c, [W], F32)
-            nc.vector.tensor_tensor(rb[:], pab[:, :W], pab[:, W:], ALU.max)
-            ub = sb("ub2_%d" % c, [S], F32)
-            scatter(ub, l_n8, pab[:, W:])
-            pieces = [(0, S)] if c < 3 else [(0, S - LAST), (S - LAST, LAST)]
-            for i, (first, count) in enumerate(pieces):
-                sn = sb("sn%d_%d" % (c, i), [count], F32)
-                nc.scalar.activation(sn[:], s[:].indirect(entries(l_n10, first, count)), ACT.Copy)
-                if i == 0:
-                    scatter(ub, l_n9, rb[:])
-                res = sb("res%d_%d" % (c, i), [count], F32)
-                nc.vector.tensor_tensor(res[:], ub[:, first : first + count], sn[:], ALU.subtract)
-                nc.sync.dma_start(out=out[c * P : (c + 1) * P, first : first + count], in_=res[:])
+        for c in range(TILES):
+            pab2 = fetch_pairs("pairs_s%d" % c, s_tiles[c], l_n6, l_n7)
+            rb2 = sb("rb2_%d" % c, [W], F32)
+            nc.vector.tensor_tensor(rb2[:], pab2[:, :W], pab2[:, W:], ALU.max)
+            ub2 = sb("ub2_%d" % c, [S], F32)
+            scatter(ub2, l_n8, pab2[:, W:])
+            pieces = [(0, S)] if c < TILES - 1 else [(0, S - LAST), (S - LAST, LAST)]
+            for first, count in pieces:
+                s_n10 = sb("s_n10_%d_%d" % (c, first), [count], F32)
+                nc.scalar.activation(s_n10[:], s_tiles[c][:].indirect(entries(l_n10, first, count)), ACT.Copy)
+                if first == 0:
+                    scatter(ub2, l_n9, rb2[:])
+                res = sb("res%d_%d" % (c, first), [count], F32)
+                nc.vector.tensor_tensor(res[:], ub2[:, first : first + count], s_n10[:], ALU.subtract)
+                nc.sync.dma_start(out=out[block(c), first : first + count], in_=res[:])

from contextlib import ExitStack

import concourse.mybir as mybir
from concourse.masks import make_identity

F32 = mybir.dt.float32
BF16 = mybir.dt.bfloat16
I32 = mybir.dt.int32
U32 = mybir.dt.uint32
U16 = mybir.dt.uint16
U8 = mybir.dt.uint8
FP8X4 = mybir.dt.float8_e4m3fn_x4
ALU = mybir.AluOpType
ACT = mybir.ActivationFunctionType

P = 128
K, T, S, G, H, W, C = 512, 1024, 256, 2048, 512, 128, 512
TILES = 4
HALF = H // 2
SIXTEENTH = 0.0625
SPARE = 16
LAST = 64
FLOPS = 2 * K * H * S * 3 + 2 * K * C * S

SHARED_AT = {
    "pairs_h1": 0, "codes_late": 0, "z0_0": 0, "z0_1": 512, "picked_cand": 2048,
    "codes_early0": 3072, "picked_late": 3072,
    "pairs_h3": 5888, "codes_cand": 4096, "z1_0": 6144, "z1_1": 6656,
}


def tile_picked_mtthzceordcpsw_none_p_kernel(
    tc, x_words, x_scales, d_words, d_scales, sl, th, gs,
    offs, k1, two, k2, hz, k3, n1, n2, n3, n4, n5, cand, n6, n7, n8, n9, n10, out,
):
    nc = tc.nc
    with ExitStack() as ctx:
        lists = ctx.enter_context(tc.tile_pool(name="lists", bufs=1))
        keep = ctx.enter_context(tc.tile_pool(name="keep", bufs=1))
        shared = ctx.enter_context(tc.tile_pool(name="shared", bufs=1))
        psum = ctx.enter_context(tc.psum_pool(name="psum", bufs=1))

        def sb(name, cols, dtype):
            if name in SHARED_AT:
                return shared.tile([P] + cols, dtype, name=name, tag=name, align_bytes=64, offset=SHARED_AT[name])
            return keep.tile([P] + cols, dtype, name=name, tag=name, align_bytes=64)

        def bank(name, cols, number):
            return psum.tile([P] + cols, F32, name=name, tag="bank%d" % number)

        def block(i, width=P):
            return slice(i * width, (i + 1) * width)

        def load_list(name, ap):
            t = lists.tile(list(ap.shape), U16, name=name)
            nc.sync.dma_start(t[:], ap)
            return t

        def entries(lst, first, count):
            return lst[:, first // 16 : (first + count) // 16]

        def zero_bytes(t):
            nc.vector.memset(t[:].bitcast(U32), 0)

        def place_scale_rows(queue, plane, picked):
            for r in range(4):
                queue.dma_start(out=plane[r:P:32, :].bitcast(I32), in_=picked[8 * r : P : 32, :].bitcast(I32))

        def mx_pass(acc, lhs_words, lhs_plane, rhs_words, rhs_plane, start, stop):
            nc.tensor.matmul_mx(
                acc, lhsT=lhs_words.bitcast(FP8X4), lhsT_scale=lhs_plane,
                rhs=rhs_words.bitcast(FP8X4), rhs_scale=rhs_plane, start=start, stop=stop,
            )

        xs = sb("xs", [T], U8)
        ds = sb("ds", [G], U8)
        zero_bytes(xs)
        zero_bytes(ds)
        nc.scalar.dma_start(out=xs[0:P:8, :].bitcast(I32), in_=x_scales[0].bitcast(I32))
        l_hz = load_list("l_hz", hz)
        nc.scalar.dma_start(out=ds[0:P:8, :].bitcast(I32), in_=d_scales[0].bitcast(I32))
        l_k = [load_list("l_k1", k1), load_list("l_k2", k2), load_list("l_k3", k3)]
        l_x = [load_list("l_offs", offs), load_list("l_two", two), l_hz]
        xw = sb("xw", [T], U32)
        dw = sb("dw", [G], U32)
        nc.sync.dma_start(out=xw[:].bitcast(I32), in_=x_words[0].rearrange("p n t -> p (n t)").bitcast(I32))
        nc.sync.dma_start(out=dw[:].bitcast(I32), in_=d_words[0].rearrange("p n t -> p (n t)").bitcast(I32))
        l_n1, l_n2, l_n3, l_n4, l_n5 = [load_list("l_n%d" % (i + 1), a) for i, a in enumerate((n1, n2, n3, n4, n5))]
        l_cand = load_list("l_cand", cand)
        l_n6, l_n7, l_n8, l_n9, l_n10 = [load_list("l_n%d" % (i + 6), a) for i, a in enumerate((n6, n7, n8, n9, n10))]

        warm = sb("warm", [1], F32)
        warm_out = sb("warm_out", [1], F32)
        nc.vector.memset(warm[:], 0.0)
        nc.scalar.activation(warm_out[:], warm[:], ACT.Sigmoid)

        plane_early = sb("plane_early", [3 * S + 3 * HALF], U8)
        plane_late = sb("plane_late", [3 * HALF], U8)
        plane_cand = sb("plane_cand", [C], U8)
        for plane in (plane_early, plane_late, plane_cand):
            zero_bytes(plane)

        ub_tiles = [sb("ub%d" % a, [2 * S if a < TILES - 1 else S], F32) for a in range(TILES)]
        s_tiles = [sb("s%d" % c, [S + SPARE], F32) for c in range(TILES)]
        for t in ub_tiles[:-1] + s_tiles:
            nc.vector.memset(t[:, S:], 0.0)

        ident = sb("ident", [P], F32)
        make_identity(nc, ident[:])
        row_values = []
        with nc.allow_non_contiguous_dma(reason="one float32 value a row"):
            for name, ap in (("sl_t", sl), ("th_t", th), ("gs_t", gs)):
                t = sb(name, [TILES], F32)
                nc.gpsimd.dma_start(out=t[:], in_=ap.rearrange("(a p) o -> p (a o)", p=P))
                row_values.append(t)
        sl_t, th_t, gs_t = row_values

        picked_early = sb("picked_early", [3 * S + 3 * HALF], U8)
        nc.vector.tensor_copy(picked_early[:, block(2, S)], xs[:].indirect(l_x[2][:]))
        for m in range(3):
            nc.vector.tensor_copy(picked_early[:, block(3 + m, HALF)], ds[:].indirect(entries(l_k[m], 0, HALF)))
        for m in range(2):
            nc.vector.tensor_copy(picked_early[:, block(m, S)], xs[:].indirect(l_x[m][:]))
        place_scale_rows(nc.scalar, plane_early, picked_early)

        x_codes = sb("x_codes", [3 * S], U32)
        for m in range(3):
            nc.vector.tensor_copy(x_codes[:, block(m, S)], xw[:].indirect(l_x[m][:]))
        codes_early = []
        for m in range(3):
            t = sb("codes_early%d" % m, [HALF], U32)
            nc.vector.tensor_copy(t[:], dw[:].indirect(entries(l_k[m], 0, HALF)))
            codes_early.append(t[:])

        sl_th = sb("sl_th", [TILES], F32)
        nbias = sb("nbias", [TILES], F32)
        nc.gpsimd.tensor_tensor(sl_th[:], sl_t[:], th_t[:], ALU.mult)
        nc.gpsimd.tensor_scalar(nbias[:], sl_th[:], -1.0, 0.0, ALU.mult, ALU.add)

        def first_product(numbers, codes, planes):
            accs = [bank("h_acc%d" % a, [S], a) for a in numbers]
            for m in range(3):
                for i in range(2):
                    mx_pass(
                        accs[i][:], codes[m][:, block(i)], planes[m][:, block(i)],
                        x_codes[:, block(m, S)], plane_early[:, block(m, S)], m == 0, m == 2,
                    )
            return accs

        def fetch_pairs(name, window, first_list, second_list):
            t = sb(name, [2 * W], F32)
            nc.scalar.activation(t[:, W:], window[:].indirect(second_list[:]), ACT.Copy)
            nc.scalar.activation(t[:, :W], window[:].indirect(first_list[:]), ACT.Copy)
            return t

        def scatter(window, lst, values):
            nc.scalar.activation(window[:].indirect(lst[:]), values, ACT.Copy)

        def sort_pairs(numbers):
            results = []
            for a in numbers:
                pab = fetch_pairs("pairs_h%d" % a, h_tiles[a], l_n1, l_n2)
                rab = sb("ordered%d" % a, [2 * W], F32)
                nc.vector.tensor_tensor(rab[:, :W], pab[:, :W], pab[:, W:], ALU.max)
                nc.vector.tensor_tensor(rab[:, W:], pab[:, :W], pab[:, W:], ALU.min)
                results.append(rab)
            return results

        def put_back(numbers, ordered):
            for a, rab in zip(numbers, ordered):
                scatter(ub_tiles[a], l_n3, rab[:, :W])
            for a, rab in zip(numbers, ordered):
                scatter(ub_tiles[a], l_n4, rab[:, W:])

        def gate(a, first, count):
            sg = sb("sg%d_%d" % (a, first), [count], F32)
            nc.scalar.activation(
                sg[:], ub_tiles[a][:].indirect(entries(l_n5, first, count)), ACT.Sigmoid,
                bias=nbias[:, a : a + 1], scale=sl_t[:, a : a + 1],
            )
            return sg

        def turned(name, src, number):
            t = bank(name, [P], number)
            nc.tensor.transpose(t[:], src, ident[:])
            return t

        z_duos = [sb("z_duos%d" % j, [2, P, 2], BF16) for j in range(2)]

        def duos_of(a, j):
            return z_duos[j][:, :, block(a, 32), :]

        def in_duo_order(rows):
            return rows.rearrange("j (p u e) -> j u p e", u=2, e=2)

        def make_z(a, sg, round_copy):
            for j in range(2):
                z = sb("z%d_%d" % (a, j), [P], F32)
                nc.vector.scalar_tensor_tensor(
                    z[:], sg[:, block(j)], gs_t[:, a : a + 1], ub_tiles[a][:, block(j)], ALU.mult, ALU.mult
                )
                z_turned = turned("z_turned%d_%d" % (a, j), z[:], 4 + j)
                round_copy(duos_of(a, j), in_duo_order(z_turned[:]))

        accs_early = first_product((0, 1), codes_early, [plane_early[:, block(3 + m, HALF)] for m in range(3)])

        picked_late = sb("picked_late", [3 * HALF], U8)
        for m in range(3):
            nc.vector.tensor_copy(picked_late[:, block(m, HALF)], ds[:].indirect(entries(l_k[m], HALF, HALF)))
        place_scale_rows(nc.sync, plane_late, picked_late)

        h_tiles = [sb("h%d" % a, [S], F32) for a in range(TILES)]
        for a in range(2):
            nc.scalar.activation(h_tiles[a][:], accs_early[a][:], ACT.Copy, scale=SIXTEENTH)
        ordered_early = sort_pairs((0, 1))

        codes_late = sb("codes_late", [3 * HALF], U32)
        for m in range(3):
            nc.vector.tensor_copy(codes_late[:, block(m, HALF)], dw[:].indirect(entries(l_k[m], HALF, HALF)))
        accs_late = first_product(
            (2, 3), [codes_late[:, block(m, HALF)] for m in range(3)], [plane_late[:, block(m, HALF)] for m in range(3)]
        )
        for i in range(2):
            nc.vector.tensor_scalar(h_tiles[2 + i][:], accs_late[i][:], SIXTEENTH, None, ALU.mult)
        picked_cand = sb("picked_cand", [C], U8)
        nc.vector.tensor_copy(picked_cand[:], xs[:].indirect(l_cand[:]))
        place_scale_rows(nc.sync, plane_cand, picked_cand)

        put_back((0, 1), ordered_early)
        early_sg = [gate(a, 0, S) for a in range(2)]
        make_z(0, early_sg[0], nc.vector.tensor_copy)
        ordered_late = sort_pairs((2, 3))
        make_z(1, early_sg[1], nc.vector.tensor_copy)
        codes_cand = sb("codes_cand", [C], U32)
        nc.vector.tensor_copy(codes_cand[:], xw[:].indirect(l_cand[:]))

        put_back((2, 3), ordered_late)
        weighted = sb("weighted", [S], F32)
        nc.vector.tensor_scalar(weighted[:], ub_tiles[3][:], gs_t[:, 3:4], None, ALU.mult)
        weighted_turned = []
        for j in range(2):
            turned_bank = turned("weighted_bank%d" % j, weighted[:, block(j)], 6 + j)
            t = sb("weighted_turned%d" % j, [P], F32)
            nc.vector.tensor_copy(t[:], turned_bank[:])
            weighted_turned.append(t)
        make_z(2, gate(2, 0, S), nc.scalar.copy)
        for j in range(2):
            sg_turned = turned("sg_turned%d" % j, gate(3, j * P, P)[:], 1 + j)
            nc.vector.tensor_tensor(
                duos_of(3, j), in_duo_order(sg_turned[:]), in_duo_order(weighted_turned[j][:]), ALU.mult
            )

        z_codes = sb("z_codes", [S], U32)
        z_plane = sb("z_plane", [S], U8)

        def scores(acc, c, cols):
            mx_pass(acc, codes_cand[:, block(c)], plane_cand[:, block(c)], z_codes[:, cols], z_plane[:, cols], True, True)

        for j in range(2):
            z_back = bank("z_back%d" % j, [2, P], 6 + j)
            for u in range(2):
                duos = z_duos[j][:, u, :, :].rearrange("j p e -> j (p e)").bitcast(F32)
                nc.tensor.transpose(z_back[:, u, :], duos, ident[:])
            z_rows = sb("z_rows%d" % j, [4 * P], BF16)
            nc.scalar.copy(z_rows[:].bitcast(F32).rearrange("p (j u) -> p j u", u=2), z_back[:].rearrange("p u j -> p j u"))
            nc.vector.quantize_mx(z_codes[:, block(j)].bitcast(FP8X4), z_plane[:, block(j)], z_rows[:])
            half_acc = bank("s0_acc%d" % j, [P], (6, 0)[j])
            scores(half_acc[:], 0, block(j))
            nc.scalar.activation(s_tiles[0][:, block(j)], half_acc[:], ACT.Copy, scale=SIXTEENTH)

        for c in range(1, TILES):
            acc = bank("s_acc%d" % c, [S], c)
            scores(acc[:], c, slice(0, S))
            nc.vector.tensor_scalar(s_tiles[c][:, :S], acc[:], SIXTEENTH, None, ALU.mult)

        for c in range(TILES):
            pab2 = fetch_pairs("pairs_s%d" % c, s_tiles[c], l_n6, l_n7)
            rb2 = sb("rb2_%d" % c, [W], F32)
            nc.vector.tensor_tensor(rb2[:], pab2[:, :W], pab2[:, W:], ALU.max)
            ub2 = sb("ub2_%d" % c, [S], F32)
            scatter(ub2, l_n8, pab2[:, W:])
            pieces = [(0, S)] if c < TILES - 1 else [(0, S - LAST), (S - LAST, LAST)]
            for first, count in pieces:
                s_n10 = sb("s_n10_%d_%d" % (c, first), [count], F32)
                nc.scalar.activation(s_n10[:], s_tiles[c][:].indirect(entries(l_n10, first, count)), ACT.Copy)
                if first == 0:
                    scatter(ub2, l_n9, rb2[:])
                res = sb("res%d_%d" % (c, first), [count], F32)
                nc.vector.tensor_tensor(res[:], ub2[:, first : first + count], s_n10[:], ALU.subtract)
                nc.sync.dma_start(out=out[block(c), first : first + count], in_=res[:])
